import numpy as np
import ml_dtypes


def mxq(x, axis, fmt="e4m3"):
    dtype, down = {"e4m3": (ml_dtypes.float8_e4m3fn, 7), "e5m2": (ml_dtypes.float8_e5m2, 14)}[fmt]
    v = np.moveaxis(np.asarray(x, np.float32).astype(ml_dtypes.bfloat16).astype(np.float64), axis, -1)
    blocks = v.reshape(v.shape[:-1] + (-1, 32))
    amax = np.abs(blocks).max(-1, keepdims=True)
    byte = np.maximum(np.where(amax > 0, np.frexp(amax)[1] - 1 + 127, 0) - down, 1)
    scale = np.exp2(byte - 127.0)
    codes = (blocks / scale).astype(np.float32).astype(dtype).astype(np.float64)
    return np.moveaxis((codes * scale).reshape(v.shape), -1, axis)


WIDE = False


def mx_kscale(k):
    if not WIDE:
        return np.ones(k)
    levels = np.array([30, -30])
    if k % 512:
        return np.exp2(np.random.permutation(np.resize(levels, k // 32))).repeat(32)
    a = np.empty((k // 512, 16))
    for p in range(k // 512):
        a[p, :8] = np.random.permutation(np.resize(levels, 8))
        for g in range(8):
            far = levels[np.abs(levels - a[p, g]) >= 10]
            a[p, g + 8] = far[np.random.randint(len(far))]
    return np.exp2(a.ravel()).repeat(32)


def f64(x):
    return np.asarray(x).astype(np.float64)


def striped(idx):
    return np.tile(np.asarray(idx).reshape(-1, 16).T, (8, 1)).astype(np.uint16)


def unstriped(offs):
    return offs[:16].T.reshape(-1).astype(np.int64)


E2M1 = np.array([0.0, 0.5, 1.0, 1.5, 2.0, 3.0, 4.0, 6.0, -0.0, -0.5, -1.0, -1.5, -2.0, -3.0, -4.0, -6.0])


def pack_weight(w, fmt):
    k, n = w.shape
    w = f64(np.asarray(w, np.float32).astype(ml_dtypes.bfloat16)).reshape(k // 32, 32, n)
    amax = np.abs(w).max(1)
    if fmt in ("e4m3", "e5m2"):
        byte = np.frexp(amax)[1] - 1 + 127 - (7 if fmt == "e4m3" else 14)
    else:
        mant, ex = np.frexp(amax / 6.0)
        byte = np.where(mant > 0.5, ex, ex - 1) + 127
    byte = np.clip(np.where(amax > 0, byte, 1), 1, 254)
    scaled = (w * np.exp2(127.0 - byte)[:, None, :]).reshape(k, n).astype(np.float32)
    by_word = np.ascontiguousarray(scaled.reshape(k // 512, 128, 4, n).transpose(0, 1, 3, 2))
    if fmt in ("e4m3", "e5m2"):
        words = by_word.astype(ml_dtypes.float8_e4m3fn if fmt == "e4m3" else ml_dtypes.float8_e5m2).view(np.uint8)
    else:
        c = by_word.astype(ml_dtypes.float4_e2m1fn).view(np.uint8) & 0xF
        words = (c[..., 0::2] | (c[..., 1::2] << 4)).reshape(k // 512, 128, 2 * n)
    return np.ascontiguousarray(words), np.ascontiguousarray(byte.astype(np.uint8).reshape(k // 512, 16, n))


def unpack_weight(words, scales, fmt):
    g, _, n = scales.shape
    words = np.ascontiguousarray(words).reshape(g, 128, n, -1)
    if fmt in ("e4m3", "e5m2"):
        vals = words.view(ml_dtypes.float8_e4m3fn if fmt == "e4m3" else ml_dtypes.float8_e5m2).astype(np.float64)
    else:
        nib = np.empty((g, 128, n, 4), np.uint8)
        nib[..., 0::2] = words & 0xF
        nib[..., 1::2] = words >> 4
        vals = E2M1[nib]
    vals = vals * np.repeat(np.exp2(scales.astype(np.float64) - 127.0), 8, axis=1)[..., None]
    return vals.transpose(0, 1, 3, 2).reshape(g * 512, n)


K, F, T, Z, J, R, O, N = 512, 512, 1024, 1024, 256, 512, 128, 256


def setup_inputs():
    n = np.random.standard_normal
    idx = np.random.permutation(T)[:J]
    idx2 = np.random.permutation(Z)[:J]
    idx3 = np.random.permutation(J)[:O]
    idx4 = np.random.permutation(J)[:O]
    idx5 = np.random.permutation(J)[:O]
    idx6 = np.random.permutation(T)[:O]
    fk = mx_kscale(K)
    fr = mx_kscale(R)
    ff = mx_kscale(F)
    xtp = pack_weight(n((K, T)) / fk[:, None], "e2m1")
    wp = pack_weight(n((K, R)) * 1 / np.sqrt(K) * fk[:, None] * fr, "e5m2")
    xop = pack_weight(n((F, Z)) / ff[:, None], "e5m2")
    w0p = pack_weight(n((F, R)) * 1 / np.sqrt(F) * ff[:, None] * fr, "e4m3")
    wbp = pack_weight(n((R, N)) * 1 / np.sqrt(R) / fr[:, None], "e4m3")
    wsp = pack_weight(n((K, N)) * 1 / np.sqrt(K) * fk[:, None], "e4m3")
    return {
        "xt_words": xtp[0],
        "xt_scales": xtp[1],
        "w_words": wp[0],
        "w_scales": wp[1],
        "xo_words": xop[0],
        "xo_scales": xop[1],
        "w0_words": w0p[0],
        "w0_scales": w0p[1],
        "wb_words": wbp[0],
        "wb_scales": wbp[1],
        "ws_words": wsp[0],
        "ws_scales": wsp[1],
        "offs": striped(idx),
        "offs2": striped(idx2),
        "offs3": striped(idx3),
        "offs4": striped(idx4),
        "offs5": striped(idx5),
        "offs6": striped(idx6),
    }


def reference(xt_words, xt_scales, w_words, w_scales, xo_words, xo_scales, w0_words, w0_scales, wb_words, wb_scales, ws_words, ws_scales, offs, offs2, offs3, offs4, offs5, offs6):
    idx = unstriped(offs)
    idx2 = unstriped(offs2)
    idx3 = unstriped(offs3)
    idx4 = unstriped(offs4)
    idx5 = unstriped(offs5)
    idx6 = unstriped(offs6)
    xtu = unpack_weight(xt_words, xt_scales, "e2m1")
    wu = unpack_weight(w_words, w_scales, "e5m2")
    xou = unpack_weight(xo_words, xo_scales, "e5m2")
    w0u = unpack_weight(w0_words, w0_scales, "e4m3")
    wbu = unpack_weight(wb_words, wb_scales, "e4m3")
    wsu = unpack_weight(ws_words, ws_scales, "e4m3")
    xtidxg = xtu[:, idx]
    xoidx2g = xou[:, idx2]
    a = wu.T @ xtidxg + w0u.T @ xoidx2g
    lo = np.minimum(a[:, idx3], a[:, idx4])
    hi = np.maximum(a[:, idx3], a[:, idx4])
    hid = np.maximum(lo, np.minimum(hi, a[:, idx5]))
    hidq = mxq(hid, 0, "e5m2")
    xtidx6g = xtu[:, idx6]
    y = wbu.T @ hidq + wsu.T @ xtidx6g
    return y

@@ -1,0 +1,189 @@
+from contextlib import ExitStack
+
+import concourse.mybir as mybir
+
+K, F, T, Z, J, R, O, N = 512, 512, 1024, 1024, 256, 512, 128, 256
+FLOPS = 2 * R * J * (K + F) + 2 * N * O * (R + K)
+
+F32 = mybir.dt.float32
+BF16 = mybir.dt.bfloat16
+I32 = mybir.dt.int32
+U32 = mybir.dt.uint32
+U16 = mybir.dt.uint16
+U8 = mybir.dt.uint8
+E4M3 = mybir.dt.float8_e4m3fn_x4
+E5M2 = mybir.dt.float8_e5m2_x4
+E2M1 = mybir.dt.float4_e2m1fn_x4
+MIN = mybir.AluOpType.min
+MAX = mybir.AluOpType.max
+COPY = mybir.ActivationFunctionType.Copy
+
+P = 128
+PACK = 4
+
+
+def tile_list_middleofthree_bank_further_plain_kernel(
+    tc, xt_words, xt_scales, w_words, w_scales, xo_words, xo_scales, w0_words, w0_scales,
+    wb_words, wb_scales, ws_words, ws_scales, offs, offs2, offs3, offs4, offs5, offs6, out,
+):
+    nc = tc.nc
+    with ExitStack() as ctx:
+        sb = ctx.enter_context(tc.tile_pool(name="sb", bufs=1))
+        ps = ctx.enter_context(tc.psum_pool(name="ps", bufs=1))
+
+        def sbuf(name, shape, dtype):
+            return sb.tile(shape, dtype, name=name, align_bytes=64)
+
+        def load_list(name, src):
+            tile = sbuf(name, list(src.shape), U16)
+            nc.sync.dma_start(tile[:], src)
+            return tile
+
+        def load_fp8_words(name, src, dtype):
+            tile = sbuf(name, [P, src.shape[2]], dtype)
+            nc.sync.dma_start(tile[:].bitcast(I32), src[0].rearrange("p n t -> p (n t)").bitcast(I32))
+            return tile
+
+        def zeroed_plane(name, width, engine):
+            tile = sbuf(name, [P, width], U8)
+            engine.memset(tile[:].bitcast(I32), 0)
+            return tile
+
+        def load_scales(plane, src, quadrants):
+            for q in quadrants:
+                nc.sync.dma_start(plane[32 * q : 32 * q + 4, :].bitcast(I32), src[0, 4 * q : 4 * q + 4, :].bitcast(I32))
+
+        def gather_vector(name, window, offsets, count, dtype):
+            tile = sbuf(name, [P, count], dtype)
+            nc.vector.tensor_copy(tile[:], window[:].indirect(offsets[:]))
+            return tile
+
+        def deal_columns(name, src, dtype, line):
+            tile = sbuf(name, [P, R], dtype)
+            nc.vector.tensor_copy(
+                tile[:].rearrange("p (t c i) -> p c t i", t=PACK, i=line),
+                src[:].rearrange("p (c i t) -> p c t i", t=PACK, i=line),
+            )
+            return tile
+
+        xt_s = zeroed_plane("xt_s", T, nc.gpsimd)
+        w_s = zeroed_plane("w_s", R, nc.gpsimd)
+        xo_s = zeroed_plane("xo_s", Z, nc.vector)
+        w0_s = zeroed_plane("w0_s", R, nc.vector)
+        ws_s = zeroed_plane("ws_s", N, nc.gpsimd)
+        wb_s = zeroed_plane("wb_s", N, nc.gpsimd)
+
+        idx = load_list("idx", offs)
+        idx2 = load_list("idx2", offs2)
+        load_scales(xt_s, xt_scales, range(4))
+        xt_w = sbuf("xt_w", [P, T], U16)
+        nc.sync.dma_start(xt_w[:].bitcast(I32), xt_words[0].bitcast(I32))
+        w_w = load_fp8_words("w_w", w_words, I32)
+        load_scales(w_s, w_scales, range(4))
+        load_scales(xo_s, xo_scales, range(2))
+        xo_w = load_fp8_words("xo_w", xo_words, U32)
+        w0_w = load_fp8_words("w0_w", w0_words, I32)
+        load_scales(xo_s, xo_scales, range(2, 4))
+        load_scales(w0_s, w0_scales, range(4))
+        idx3 = load_list("idx3", offs3)
+        idx4 = load_list("idx4", offs4)
+        idx6 = load_list("idx6", offs6)
+        idx5 = load_list("idx5", offs5)
+        ws_w = load_fp8_words("ws_w", ws_words, I32)
+        wb_w = load_fp8_words("wb_w", wb_words, I32)
+        load_scales(ws_s, ws_scales, range(4))
+        load_scales(wb_s, wb_scales, range(4))
+
+        tok_s = gather_vector("tok_s", xt_s, idx, J, U8)
+        tok_w = gather_vector("tok_w", xt_w, idx, J, U16)
+        w_wd = deal_columns("w_wd", w_w, I32, 4)
+        w_sd = deal_columns("w_sd", w_s, U8, 16)
+        note_w = gather_vector("note_w", xo_w, idx2, J, U32)
+        w0_wd = deal_columns("w0_wd", w0_w, I32, 4)
+        note_s = gather_vector("note_s", xo_s, idx2, J, U8)
+        w0_sd = deal_columns("w0_sd", w0_s, U8, 16)
+
+        a_ps = [ps.tile([P, J], F32, name=f"a_ps{t}") for t in range(PACK)]
+        for t in range(PACK):
+            cols = slice(t * P, (t + 1) * P)
+            nc.tensor.matmul_mx(
+                out=a_ps[t][:], lhsT=w_wd[:, cols].bitcast(E5M2), lhsT_scale=w_sd[:, cols],
+                rhs=tok_w[:].bitcast(E2M1), rhs_scale=tok_s[:], start=True, stop=False,
+            )
+        for t in range(PACK):
+            cols = slice(t * P, (t + 1) * P)
+            nc.tensor.matmul_mx(
+                out=a_ps[t][:], lhsT=w0_wd[:, cols].bitcast(E4M3), lhsT_scale=w0_sd[:, cols],
+                rhs=note_w[:].bitcast(E5M2), rhs_scale=note_s[:], start=False, stop=True,
+            )
+
+        short_w = gather_vector("short_w", xt_w, idx6, O, U16)
+        short_s = gather_vector("short_s", xt_s, idx6, O, U8)
+
+        a_sb = [sbuf(f"a_sb{t}", [P, J], F32) for t in range(PACK)]
+        first = sbuf("first", [P, PACK, O], F32)
+        second = sbuf("second", [P, PACK, O], F32)
+        third = sbuf("third", [P, PACK, O], F32)
+        lists = {0: idx3, 1: idx4, 2: idx5}
+        picked = {0: first, 1: second, 2: third}
+
+        def pick(engine, which, t):
+            window = a_sb[t][:].indirect(lists[which][:])
+            if engine == "vector":
+                nc.vector.tensor_copy(picked[which][:, t, :], window)
+            else:
+                nc.scalar.activation(picked[which][:, t, :], window, COPY)
+
+        nc.vector.tensor_copy(a_sb[0][:], a_ps[0][:])
+        nc.scalar.activation(a_sb[1][:], a_ps[1][:], COPY)
+        nc.vector.tensor_copy(a_sb[2][:], a_ps[2][:])
+        pick("scalar", 0, 0)
+        nc.scalar.activation(a_sb[3][:], a_ps[3][:], COPY)
+        pick("vector", 0, 1)
+        pick("vector", 1, 1)
+        pick("scalar", 1, 0)
+        pick("scalar", 0, 2)
+        pick("scalar", 1, 2)
+        pick("vector", 0, 3)
+        pick("vector", 1, 3)
+        for t in range(PACK):
+            pick("scalar", 2, t)
+
+        y_ps = [ps.tile([P, O], F32, name=f"y_ps{h}") for h in range(N // P)]
+        for h in range(N // P):
+            cols = slice(h * P, (h + 1) * P)
+            nc.tensor.matmul_mx(
+                out=y_ps[h][:], lhsT=ws_w[:, cols].bitcast(E4M3), lhsT_scale=ws_s[:, cols],
+                rhs=short_w[:].bitcast(E2M1), rhs_scale=short_s[:], start=True, stop=False,
+            )
+
+        lo = sbuf("lo", [P, PACK, O], F32)
+        hi = sbuf("hi", [P, PACK, O], F32)
+        mid = sbuf("mid", [P, PACK, O], F32)
+        halves = [slice(0, 2), slice(2, 4)]
+        for half in halves:
+            nc.vector.tensor_tensor(lo[:, half, :], first[:, half, :], second[:, half, :], MIN)
+            nc.vector.tensor_tensor(hi[:, half, :], first[:, half, :], second[:, half, :], MAX)
+        for half in halves:
+            nc.vector.tensor_tensor(mid[:, half, :], hi[:, half, :], third[:, half, :], MIN)
+        hid = sbuf("hid", [P, O * PACK], BF16)
+        nc.vector.tensor_tensor(
+            hid[:].rearrange("p (c i t) -> p c t i", t=PACK, i=4),
+            lo[:].rearrange("p t (c i) -> p c t i", i=4),
+            mid[:].rearrange("p t (c i) -> p c t i", i=4),
+            MAX,
+        )
+        hid_w = sbuf("hid_w", [P, O], U32)
+        hid_s = sbuf("hid_s", [P, O], U8)
+        nc.vector.quantize_mx(out=hid_w[:].bitcast(E5M2), scales=hid_s[:], in_=hid[:])
+
+        y_sb = sbuf("y_sb", [P, N // P, O], F32)
+        for h in range(N // P):
+            cols = slice(h * P, (h + 1) * P)
+            nc.tensor.matmul_mx(
+                out=y_ps[h][:], lhsT=wb_w[:, cols].bitcast(E4M3), lhsT_scale=wb_s[:, cols],
+                rhs=hid_w[:].bitcast(E5M2), rhs_scale=hid_s[:], start=False, stop=True,
+            )
+        nc.vector.tensor_copy(y_sb[:, 0, :], y_ps[0][:])
+        nc.scalar.copy(y_sb[:, 1, :], y_ps[1][:])
+        nc.sync.dma_start(out.rearrange("(h p) o -> p h o", p=P), y_sb[:])

@@ -31,8 +31,8 @@ def tile_list_middleofthree_bank_further_plain_kernel(
         sb = ctx.enter_context(tc.tile_pool(name="sb", bufs=1))
         ps = ctx.enter_context(tc.psum_pool(name="ps", bufs=1))
 
-        def sbuf(name, shape, dtype):
-            return sb.tile(shape, dtype, name=name, align_bytes=64)
+        def sbuf(name, shape, dtype, tag=None):
+            return sb.tile(shape, dtype, name=name, tag=tag or name, align_bytes=64)
 
         def load_list(name, src):
             tile = sbuf(name, list(src.shape), U16)
@@ -49,17 +49,17 @@ def tile_list_middleofthree_bank_further_plain_kernel(
             engine.memset(tile[:].bitcast(I32), 0)
             return tile
 
-        def load_scales(plane, src, quadrants):
+        def load_scales(queue, plane, src, quadrants):
             for q in quadrants:
-                nc.sync.dma_start(plane[32 * q : 32 * q + 4, :].bitcast(I32), src[0, 4 * q : 4 * q + 4, :].bitcast(I32))
+                queue.dma_start(plane[32 * q : 32 * q + 4, :].bitcast(I32), src[0, 4 * q : 4 * q + 4, :].bitcast(I32))
 
-        def gather_vector(name, window, offsets, count, dtype):
-            tile = sbuf(name, [P, count], dtype)
+        def gather_vector(name, window, offsets, count, dtype, tag=None):
+            tile = sbuf(name, [P, count], dtype, tag)
             nc.vector.tensor_copy(tile[:], window[:].indirect(offsets[:]))
             return tile
 
-        def deal_columns(name, src, dtype, line):
-            tile = sbuf(name, [P, R], dtype)
+        def deal_columns(name, src, dtype, line, tag=None):
+            tile = sbuf(name, [P, R], dtype, tag)
             nc.vector.tensor_copy(
                 tile[:].rearrange("p (t c i) -> p c t i", t=PACK, i=line),
                 src[:].rearrange("p (c i t) -> p c t i", t=PACK, i=line),
@@ -70,55 +70,57 @@ def tile_list_middleofthree_bank_further_plain_kernel(
         w_s = zeroed_plane("w_s", R, nc.gpsimd)
         xo_s = zeroed_plane("xo_s", Z, nc.vector)
         w0_s = zeroed_plane("w0_s", R, nc.vector)
-        ws_s = zeroed_plane("ws_s", N, nc.gpsimd)
-        wb_s = zeroed_plane("wb_s", N, nc.gpsimd)
+        ws_s = zeroed_plane("ws_s", N, nc.vector)
+        wb_s = zeroed_plane("wb_s", N, nc.vector)
 
         idx = load_list("idx", offs)
         idx2 = load_list("idx2", offs2)
-        load_scales(xt_s, xt_scales, range(4))
+        load_scales(nc.sync, xt_s, xt_scales, range(4))
         xt_w = sbuf("xt_w", [P, T], U16)
         nc.sync.dma_start(xt_w[:].bitcast(I32), xt_words[0].bitcast(I32))
-        w_w = load_fp8_words("w_w", w_words, I32)
-        load_scales(w_s, w_scales, range(4))
-        load_scales(xo_s, xo_scales, range(2))
         xo_w = load_fp8_words("xo_w", xo_words, U32)
+        load_scales(nc.gpsimd, w_s, w_scales, range(2, 4))
+        load_scales(nc.sync, xo_s, xo_scales, range(4))
+        load_scales(nc.sync, w_s, w_scales, range(2))
+        w_w = load_fp8_words("w_w", w_words, I32)
         w0_w = load_fp8_words("w0_w", w0_words, I32)
-        load_scales(xo_s, xo_scales, range(2, 4))
-        load_scales(w0_s, w0_scales, range(4))
+        load_scales(nc.sync, w0_s, w0_scales, range(4))
+        idx6 = load_list("idx6", offs6)
         idx3 = load_list("idx3", offs3)
         idx4 = load_list("idx4", offs4)
-        idx6 = load_list("idx6", offs6)
         idx5 = load_list("idx5", offs5)
+        load_scales(nc.sync, ws_s, ws_scales, range(4))
+        load_scales(nc.sync, wb_s, wb_scales, range(2))
+        load_scales(nc.gpsimd, wb_s, wb_scales, range(2, 4))
         ws_w = load_fp8_words("ws_w", ws_words, I32)
         wb_w = load_fp8_words("wb_w", wb_words, I32)
-        load_scales(ws_s, ws_scales, range(4))
-        load_scales(wb_s, wb_scales, range(4))
 
         tok_s = gather_vector("tok_s", xt_s, idx, J, U8)
         tok_w = gather_vector("tok_w", xt_w, idx, J, U16)
+        note_w = gather_vector("note_w", xo_w, idx2, J, U32)
+        note_s = gather_vector("note_s", xo_s, idx2, J, U8)
         w_wd = deal_columns("w_wd", w_w, I32, 4)
         w_sd = deal_columns("w_sd", w_s, U8, 16)
-        note_w = gather_vector("note_w", xo_w, idx2, J, U32)
-        w0_wd = deal_columns("w0_wd", w0_w, I32, 4)
-        note_s = gather_vector("note_s", xo_s, idx2, J, U8)
-        w0_sd = deal_columns("w0_sd", w0_s, U8, 16)
+        w0_wd = deal_columns("w0_wd", w0_w, I32, 4, "w_s")
+        w0_sd = deal_columns("w0_sd", w0_s, U8, 16, "w0_w")
 
         a_ps = [ps.tile([P, J], F32, name=f"a_ps{t}") for t in range(PACK)]
-        for t in range(PACK):
+        order = (0, 2, 3, 1)
+        for t in order:
             cols = slice(t * P, (t + 1) * P)
             nc.tensor.matmul_mx(
                 out=a_ps[t][:], lhsT=w_wd[:, cols].bitcast(E5M2), lhsT_scale=w_sd[:, cols],
                 rhs=tok_w[:].bitcast(E2M1), rhs_scale=tok_s[:], start=True, stop=False,
             )
-        for t in range(PACK):
+        for t in order:
             cols = slice(t * P, (t + 1) * P)
             nc.tensor.matmul_mx(
                 out=a_ps[t][:], lhsT=w0_wd[:, cols].bitcast(E4M3), lhsT_scale=w0_sd[:, cols],
                 rhs=note_w[:].bitcast(E5M2), rhs_scale=note_s[:], start=False, stop=True,
             )
 
-        short_w = gather_vector("short_w", xt_w, idx6, O, U16)
-        short_s = gather_vector("short_s", xt_s, idx6, O, U8)
+        short_w = gather_vector("short_w", xt_w, idx6, O, U16, "tok_w")
+        short_s = gather_vector("short_s", xt_s, idx6, O, U8, "tok_s")
 
         a_sb = [sbuf(f"a_sb{t}", [P, J], F32) for t in range(PACK)]
         first = sbuf("first", [P, PACK, O], F32)
@@ -134,20 +136,16 @@ def tile_list_middleofthree_bank_further_plain_kernel(
             else:
                 nc.scalar.activation(picked[which][:, t, :], window, COPY)
 
-        nc.vector.tensor_copy(a_sb[0][:], a_ps[0][:])
-        nc.scalar.activation(a_sb[1][:], a_ps[1][:], COPY)
-        nc.vector.tensor_copy(a_sb[2][:], a_ps[2][:])
-        pick("scalar", 0, 0)
-        nc.scalar.activation(a_sb[3][:], a_ps[3][:], COPY)
-        pick("vector", 0, 1)
-        pick("vector", 1, 1)
-        pick("scalar", 1, 0)
-        pick("scalar", 0, 2)
-        pick("scalar", 1, 2)
-        pick("vector", 0, 3)
-        pick("vector", 1, 3)
-        for t in range(PACK):
+        nc.scalar.activation(a_sb[order[0]][:], a_ps[order[0]][:], COPY)
+        for t in order[1:]:
+            nc.vector.tensor_copy(a_sb[t][:], a_ps[t][:])
+        for t in order[:3]:
+            pick("scalar", 0, t)
+            pick("scalar", 1, t)
+        for t in order[:3]:
             pick("scalar", 2, t)
+        for which in range(3):
+            pick("vector", which, order[3])
 
         y_ps = [ps.tile([P, O], F32, name=f"y_ps{h}") for h in range(N // P)]
         for h in range(N // P):

from contextlib import ExitStack

import concourse.mybir as mybir

K, F, T, Z, J, R, O, N = 512, 512, 1024, 1024, 256, 512, 128, 256
FLOPS = 2 * R * J * (K + F) + 2 * N * O * (R + K)

F32 = mybir.dt.float32
BF16 = mybir.dt.bfloat16
I32 = mybir.dt.int32
U32 = mybir.dt.uint32
U16 = mybir.dt.uint16
U8 = mybir.dt.uint8
E4M3 = mybir.dt.float8_e4m3fn_x4
E5M2 = mybir.dt.float8_e5m2_x4
E2M1 = mybir.dt.float4_e2m1fn_x4
MIN = mybir.AluOpType.min
MAX = mybir.AluOpType.max
COPY = mybir.ActivationFunctionType.Copy

P = 128
PACK = 4


def tile_list_middleofthree_bank_further_plain_kernel(
    tc, xt_words, xt_scales, w_words, w_scales, xo_words, xo_scales, w0_words, w0_scales,
    wb_words, wb_scales, ws_words, ws_scales, offs, offs2, offs3, offs4, offs5, offs6, out,
):
    nc = tc.nc
    with ExitStack() as ctx:
        sb = ctx.enter_context(tc.tile_pool(name="sb", bufs=1))
        ps = ctx.enter_context(tc.psum_pool(name="ps", bufs=1))

        def sbuf(name, shape, dtype, tag=None):
            return sb.tile(shape, dtype, name=name, tag=tag or name, align_bytes=64)

        def load_list(name, src):
            tile = sbuf(name, list(src.shape), U16)
            nc.sync.dma_start(tile[:], src)
            return tile

        def load_fp8_words(name, src, dtype):
            tile = sbuf(name, [P, src.shape[2]], dtype)
            nc.sync.dma_start(tile[:].bitcast(I32), src[0].rearrange("p n t -> p (n t)").bitcast(I32))
            return tile

        def zeroed_plane(name, width, engine):
            tile = sbuf(name, [P, width], U8)
            engine.memset(tile[:].bitcast(I32), 0)
            return tile

        def load_scales(queue, plane, src, quadrants):
            for q in quadrants:
                queue.dma_start(plane[32 * q : 32 * q + 4, :].bitcast(I32), src[0, 4 * q : 4 * q + 4, :].bitcast(I32))

        def gather_vector(name, window, offsets, count, dtype, tag=None):
            tile = sbuf(name, [P, count], dtype, tag)
            nc.vector.tensor_copy(tile[:], window[:].indirect(offsets[:]))
            return tile

        def deal_columns(name, src, dtype, line, tag=None):
            tile = sbuf(name, [P, R], dtype, tag)
            nc.vector.tensor_copy(
                tile[:].rearrange("p (t c i) -> p c t i", t=PACK, i=line),
                src[:].rearrange("p (c i t) -> p c t i", t=PACK, i=line),
            )
            return tile

        xt_s = zeroed_plane("xt_s", T, nc.gpsimd)
        w_s = zeroed_plane("w_s", R, nc.gpsimd)
        xo_s = zeroed_plane("xo_s", Z, nc.vector)
        w0_s = zeroed_plane("w0_s", R, nc.vector)
        ws_s = zeroed_plane("ws_s", N, nc.vector)
        wb_s = zeroed_plane("wb_s", N, nc.vector)

        idx = load_list("idx", offs)
        idx2 = load_list("idx2", offs2)
        load_scales(nc.sync, xt_s, xt_scales, range(4))
        xt_w = sbuf("xt_w", [P, T], U16)
        nc.sync.dma_start(xt_w[:].bitcast(I32), xt_words[0].bitcast(I32))
        xo_w = load_fp8_words("xo_w", xo_words, U32)
        load_scales(nc.gpsimd, w_s, w_scales, range(2, 4))
        load_scales(nc.sync, xo_s, xo_scales, range(4))
        load_scales(nc.sync, w_s, w_scales, range(2))
        w_w = load_fp8_words("w_w", w_words, I32)
        w0_w = load_fp8_words("w0_w", w0_words, I32)
        load_scales(nc.sync, w0_s, w0_scales, range(4))
        idx6 = load_list("idx6", offs6)
        idx3 = load_list("idx3", offs3)
        idx4 = load_list("idx4", offs4)
        idx5 = load_list("idx5", offs5)
        load_scales(nc.sync, ws_s, ws_scales, range(4))
        load_scales(nc.sync, wb_s, wb_scales, range(2))
        load_scales(nc.gpsimd, wb_s, wb_scales, range(2, 4))
        ws_w = load_fp8_words("ws_w", ws_words, I32)
        wb_w = load_fp8_words("wb_w", wb_words, I32)

        tok_s = gather_vector("tok_s", xt_s, idx, J, U8)
        tok_w = gather_vector("tok_w", xt_w, idx, J, U16)
        note_w = gather_vector("note_w", xo_w, idx2, J, U32)
        note_s = gather_vector("note_s", xo_s, idx2, J, U8)
        w_wd = deal_columns("w_wd", w_w, I32, 4)
        w_sd = deal_columns("w_sd", w_s, U8, 16)
        w0_wd = deal_columns("w0_wd", w0_w, I32, 4, "w_s")
        w0_sd = deal_columns("w0_sd", w0_s, U8, 16, "w0_w")

        a_ps = [ps.tile([P, J], F32, name=f"a_ps{t}") for t in range(PACK)]
        order = (0, 2, 3, 1)
        for t in order:
            cols = slice(t * P, (t + 1) * P)
            nc.tensor.matmul_mx(
                out=a_ps[t][:], lhsT=w_wd[:, cols].bitcast(E5M2), lhsT_scale=w_sd[:, cols],
                rhs=tok_w[:].bitcast(E2M1), rhs_scale=tok_s[:], start=True, stop=False,
            )
        for t in order:
            cols = slice(t * P, (t + 1) * P)
            nc.tensor.matmul_mx(
                out=a_ps[t][:], lhsT=w0_wd[:, cols].bitcast(E4M3), lhsT_scale=w0_sd[:, cols],
                rhs=note_w[:].bitcast(E5M2), rhs_scale=note_s[:], start=False, stop=True,
            )

        short_w = gather_vector("short_w", xt_w, idx6, O, U16, "tok_w")
        short_s = gather_vector("short_s", xt_s, idx6, O, U8, "tok_s")

        a_sb = [sbuf(f"a_sb{t}", [P, J], F32) for t in range(PACK)]
        first = sbuf("first", [P, PACK, O], F32)
        second = sbuf("second", [P, PACK, O], F32)
        third = sbuf("third", [P, PACK, O], F32)
        lists = {0: idx3, 1: idx4, 2: idx5}
        picked = {0: first, 1: second, 2: third}

        def pick(engine, which, t):
            window = a_sb[t][:].indirect(lists[which][:])
            if engine == "vector":
                nc.vector.tensor_copy(picked[which][:, t, :], window)
            else:
                nc.scalar.activation(picked[which][:, t, :], window, COPY)

        nc.scalar.activation(a_sb[order[0]][:], a_ps[order[0]][:], COPY)
        for t in order[1:]:
            nc.vector.tensor_copy(a_sb[t][:], a_ps[t][:])
        for t in order[:3]:
            pick("scalar", 0, t)
            pick("scalar", 1, t)
        for t in order[:3]:
            pick("scalar", 2, t)
        for which in range(3):
            pick("vector", which, order[3])

        y_ps = [ps.tile([P, O], F32, name=f"y_ps{h}") for h in range(N // P)]
        for h in range(N // P):
            cols = slice(h * P, (h + 1) * P)
            nc.tensor.matmul_mx(
                out=y_ps[h][:], lhsT=ws_w[:, cols].bitcast(E4M3), lhsT_scale=ws_s[:, cols],
                rhs=short_w[:].bitcast(E2M1), rhs_scale=short_s[:], start=True, stop=False,
            )

        lo = sbuf("lo", [P, PACK, O], F32)
        hi = sbuf("hi", [P, PACK, O], F32)
        mid = sbuf("mid", [P, PACK, O], F32)
        halves = [slice(0, 2), slice(2, 4)]
        for half in halves:
            nc.vector.tensor_tensor(lo[:, half, :], first[:, half, :], second[:, half, :], MIN)
            nc.vector.tensor_tensor(hi[:, half, :], first[:, half, :], second[:, half, :], MAX)
        for half in halves:
            nc.vector.tensor_tensor(mid[:, half, :], hi[:, half, :], third[:, half, :], MIN)
        hid = sbuf("hid", [P, O * PACK], BF16)
        nc.vector.tensor_tensor(
            hid[:].rearrange("p (c i t) -> p c t i", t=PACK, i=4),
            lo[:].rearrange("p t (c i) -> p c t i", i=4),
            mid[:].rearrange("p t (c i) -> p c t i", i=4),
            MAX,
        )
        hid_w = sbuf("hid_w", [P, O], U32)
        hid_s = sbuf("hid_s", [P, O], U8)
        nc.vector.quantize_mx(out=hid_w[:].bitcast(E5M2), scales=hid_s[:], in_=hid[:])

        y_sb = sbuf("y_sb", [P, N // P, O], F32)
        for h in range(N // P):
            cols = slice(h * P, (h + 1) * P)
            nc.tensor.matmul_mx(
                out=y_ps[h][:], lhsT=wb_w[:, cols].bitcast(E4M3), lhsT_scale=wb_s[:, cols],
                rhs=hid_w[:].bitcast(E5M2), rhs_scale=hid_s[:], start=False, stop=True,
            )
        nc.vector.tensor_copy(y_sb[:, 0, :], y_ps[0][:])
        nc.scalar.copy(y_sb[:, 1, :], y_ps[1][:])
        nc.sync.dma_start(out.rearrange("(h p) o -> p h o", p=P), y_sb[:])
